import numpy as np
import ml_dtypes


def mxq(x, axis, fmt="e4m3"):
    dtype, down = {"e4m3": (ml_dtypes.float8_e4m3fn, 7), "e5m2": (ml_dtypes.float8_e5m2, 14)}[fmt]
    v = np.moveaxis(np.asarray(x, np.float32).astype(ml_dtypes.bfloat16).astype(np.float64), axis, -1)
    blocks = v.reshape(v.shape[:-1] + (-1, 32))
    amax = np.abs(blocks).max(-1, keepdims=True)
    byte = np.maximum(np.where(amax > 0, np.frexp(amax)[1] - 1 + 127, 0) - down, 1)
    scale = np.exp2(byte - 127.0)
    codes = (blocks / scale).astype(np.float32).astype(dtype).astype(np.float64)
    return np.moveaxis((codes * scale).reshape(v.shape), -1, axis)


WIDE = False


def mx_kscale(k):
    if not WIDE:
        return np.ones(k)
    levels = np.array([10, -10, 5, -5, 0])
    if k % 512:
        return np.exp2(np.random.permutation(np.resize(levels, k // 32))).repeat(32)
    a = np.empty((k // 512, 16))
    for p in range(k // 512):
        a[p, :8] = np.random.permutation(np.resize(levels, 8))
        for g in range(8):
            far = levels[np.abs(levels - a[p, g]) >= 10]
            a[p, g + 8] = far[np.random.randint(len(far))]
    return np.exp2(a.ravel()).repeat(32)


def f64(x):
    return np.asarray(x).astype(np.float64)


def striped(idx):
    return np.tile(idx.reshape(-1, 16).T, (8, 1)).astype(np.uint16)


def unstriped(offs):
    return offs[:16].T.reshape(-1).astype(np.int64)


E2M1 = np.array([0.0, 0.5, 1.0, 1.5, 2.0, 3.0, 4.0, 6.0, -0.0, -0.5, -1.0, -1.5, -2.0, -3.0, -4.0, -6.0])


def pack_weight(w, fmt):
    k, n = w.shape
    w = f64(np.asarray(w, np.float32).astype(ml_dtypes.bfloat16)).reshape(k // 32, 32, n)
    amax = np.abs(w).max(1)
    if fmt == "e4m3":
        byte = np.frexp(amax)[1] - 1 + 127 - 7
    else:
        mant, ex = np.frexp(amax / 6.0)
        byte = np.where(mant > 0.5, ex, ex - 1) + 127
    byte = np.clip(np.where(amax > 0, byte, 1), 1, 254)
    scaled = (w * np.exp2(127.0 - byte)[:, None, :]).reshape(k, n).astype(np.float32)
    by_word = np.ascontiguousarray(scaled.reshape(k // 512, 128, 4, n).transpose(0, 1, 3, 2))
    if fmt == "e4m3":
        words = by_word.astype(ml_dtypes.float8_e4m3fn).view(np.uint8)
    else:
        c = by_word.astype(ml_dtypes.float4_e2m1fn).view(np.uint8) & 0xF
        words = (c[..., 0::2] | (c[..., 1::2] << 4)).reshape(k // 512, 128, 2 * n)
    return np.ascontiguousarray(words), np.ascontiguousarray(byte.astype(np.uint8).reshape(k // 512, 16, n))


def unpack_weight(words, scales, fmt):
    g, _, n = scales.shape
    words = np.ascontiguousarray(words).reshape(g, 128, n, -1)
    if fmt == "e4m3":
        vals = words.view(ml_dtypes.float8_e4m3fn).astype(np.float64)
    else:
        nib = np.empty((g, 128, n, 4), np.uint8)
        nib[..., 0::2] = words & 0xF
        nib[..., 1::2] = words >> 4
        vals = E2M1[nib]
    vals = vals * np.repeat(np.exp2(scales.astype(np.float64) - 127.0), 8, axis=1)[..., None]
    return vals.transpose(0, 1, 3, 2).reshape(g * 512, n)


def gelu(v):
    return 0.5 * v * (1.0 + np.tanh(np.sqrt(2.0 / np.pi) * (v + 0.044715 * v**3)))


K, T, E, C, H, N = 512, 3072, 8, 256, 512, 128


def by_expert(wq, xq):
    return np.concatenate([wq[e].T @ xq[:, e * C:(e + 1) * C] for e in range(E)], axis=1)


def setup_inputs():
    n = np.random.standard_normal
    s = mx_kscale(K)[:, None]
    u = mx_kscale(H)
    w1 = [pack_weight(m, "e2m1") for m in n((E, K, H)) / np.sqrt(K) / s[None]]
    w3 = [pack_weight(m, "e2m1") for m in n((E, K, H)) / np.sqrt(K) / s[None] * u[None, None, :]]
    w2 = [pack_weight(m, "e2m1") for m in n((E, H, N)) / np.sqrt(H) / u[None, :, None]]
    return {
        "xT": (n((K, T)) * s).astype(np.float32),
        "xr": n((N, T)).astype(np.float32),
        "w1_words": np.stack([m[0] for m in w1]),
        "w1_scales": np.stack([m[1] for m in w1]),
        "w3_words": np.stack([m[0] for m in w3]),
        "w3_scales": np.stack([m[1] for m in w3]),
        "w2_words": np.stack([m[0] for m in w2]),
        "w2_scales": np.stack([m[1] for m in w2]),
        "gate": np.tile(np.random.uniform(0.2, 1.0, E * C), (N, 1)).astype(np.float32),
        "offs": striped(np.random.permutation(T)[:E * C]),
    }


def reference(xT, xr, w1_words, w1_scales, w3_words, w3_scales, w2_words, w2_scales, gate, offs):
    idx = unstriped(offs)
    w1 = np.stack([unpack_weight(w1_words[e], w1_scales[e], "e2m1") for e in range(E)])
    w3 = np.stack([unpack_weight(w3_words[e], w3_scales[e], "e2m1") for e in range(E)])
    w2 = np.stack([unpack_weight(w2_words[e], w2_scales[e], "e2m1") for e in range(E)])
    xq = mxq(f64(xT)[:, idx], 0, "e4m3")
    h = gelu(by_expert(w1, xq))
    h = h * by_expert(w3, xq)
    y = by_expert(w2, mxq(h, 0, "e4m3"))
    out = f64(xr).copy()
    out[:, idx] += f64(gate) * y
    return out

@@ -1,0 +1,224 @@
+from contextlib import ExitStack
+
+import concourse.mybir as mybir
+from concourse.masks import make_identity
+
+F32 = mybir.dt.float32
+BF16 = mybir.dt.bfloat16
+I32 = mybir.dt.int32
+U32 = mybir.dt.uint32
+U16 = mybir.dt.uint16
+U8 = mybir.dt.uint8
+FP8X4 = mybir.dt.float8_e4m3fn_x4
+FP4X4 = mybir.dt.float4_e2m1fn_x4
+GELU = mybir.ActivationFunctionType.Gelu_apprx_tanh
+MULT = mybir.AluOpType.mult
+ADD = mybir.AluOpType.add
+
+P = 128
+K, T, E, C, H, N = 512, 3072, 8, 256, 512, 128
+S = E * C
+SLICE = 512
+FLOPS = 2 * S * (2 * K * H + H * N)
+
+
+def tile_moe_res_glu_gelu_kernel(
+    tc, xT, xr, w1_words, w1_scales, w3_words, w3_scales, w2_words, w2_scales, gate, offs, out
+):
+    nc = tc.nc
+    x_rows = xT.rearrange("(p j) t -> p j t", j=4)
+    slices = S // SLICE
+
+    with ExitStack() as ctx:
+        keep = ctx.enter_context(tc.tile_pool(name="keep", bufs=1))
+        raw_pool = ctx.enter_context(tc.tile_pool(name="raw", bufs=5))
+        slot_pool = ctx.enter_context(tc.tile_pool(name="slots", bufs=4))
+        work = ctx.enter_context(tc.tile_pool(name="work", bufs=4))
+        psum_a = ctx.enter_context(tc.psum_pool(name="psum_a", bufs=2))
+        psum_b = ctx.enter_context(tc.psum_pool(name="psum_b", bufs=4))
+        psum_t = ctx.enter_context(tc.psum_pool(name="psum_t", bufs=1))
+        psum_y = ctx.enter_context(tc.psum_pool(name="psum_y", bufs=1))
+
+        offsets = keep.tile([P, S // 16], U16, name="offsets")
+        pairs = [keep.tile([P, 2 * T], BF16, name=f"pairs{u}", align_bytes=64) for u in range(2)]
+        w1_codes = keep.tile([P, E * 2 * H], U8, name="w1_codes", align_bytes=64)
+        w3_codes = keep.tile([P, E * 2 * H], U8, name="w3_codes", align_bytes=64)
+        w2_codes = keep.tile([P, E * 2 * N], U8, name="w2_codes", align_bytes=64)
+        w1_plane = keep.tile([P, E * H], U8, name="w1_plane", align_bytes=64)
+        w3_plane = keep.tile([P, E * H], U8, name="w3_plane", align_bytes=64)
+        w2_plane = keep.tile([P, E * N], U8, name="w2_plane", align_bytes=64)
+        gates = keep.tile([P, S], F32, name="gates")
+        residual = keep.tile([P, T], F32, name="residual")
+        scattered = keep.tile([P, T], F32, name="scattered")
+        identity = keep.tile([P, P], F32, name="identity")
+        warm = keep.tile([P, 1], F32, name="warm")
+
+        nc.vector.memset(warm[:], 0.0)
+        nc.scalar.activation(warm[:], warm[:], GELU)
+        for plane in (w1_plane, w3_plane, w2_plane):
+            nc.gpsimd.memset(plane[:].bitcast(I32), 0)
+        make_identity(nc, identity[:])
+        nc.gpsimd.memset(scattered[:], 0.0)
+
+        def load_and_cast(u, c0, c1, split):
+            width = c1 - c0
+            raw = raw_pool.tile([P, 2, width], F32, name="raw")
+            nc.sync.dma_start(out=raw[:], in_=x_rows[:, 2 * u : 2 * u + 2, c0:c1])
+            dst = pairs[u][:].rearrange("p (t e) -> p t e", e=2)
+            source = raw[:].rearrange("p e t -> p t e")
+            if split > 0:
+                nc.scalar.copy(out=dst[:, c0 : c0 + split, :], in_=source[:, 0:split, :])
+            if split < width:
+                nc.vector.tensor_copy(out=dst[:, c0 + split : c1, :], in_=source[:, split:width, :])
+
+        def gather(s, u, dest):
+            nc.vector.tensor_copy(
+                dest[:, u * 2 * SLICE : (u + 1) * 2 * SLICE].bitcast(U32),
+                pairs[u][:].bitcast(U32).indirect(offsets[:, s * (SLICE // 16) : (s + 1) * (SLICE // 16)]),
+            )
+
+        load_and_cast(0, 0, 1024, 512)
+        nc.sync.dma_start(offsets[:], offs)
+        load_and_cast(0, 1024, 2048, 512)
+        load_and_cast(0, 2048, 3072, 384)
+        gathered = [slot_pool.tile([P, 4 * SLICE], BF16, name="gathered", align_bytes=64) for s in range(slices)]
+        for s in range(slices):
+            gather(s, 0, gathered[s])
+        load_and_cast(1, 0, 1024, 1024)
+        load_and_cast(1, 1024, 2048, 1024)
+        load_and_cast(1, 2048, 2816, 0)
+        load_and_cast(1, 2816, 3072, 0)
+
+        def load_scales(plane, scales):
+            rows = scales.rearrange("e s (q r) i -> r q (e s) i", r=4)
+            for r in range(4):
+                nc.sync.dma_start(
+                    out=plane[r:P:32, :].bitcast(I32).rearrange("q (e i) -> q e i", e=E),
+                    in_=rows[r].bitcast(I32),
+                )
+
+        def load_words(codes, words, e0, e1):
+            wide = words.shape[3]
+            nc.sync.dma_start(
+                out=codes[:, e0 * wide : e1 * wide].bitcast(I32).rearrange("p (e b) -> p e b", e=e1 - e0),
+                in_=words[e0:e1].rearrange("e s p b -> p (e s) b").bitcast(I32),
+            )
+
+        load_scales(w1_plane, w1_scales)
+        load_scales(w3_plane, w3_scales)
+        load_words(w1_codes, w1_words, 0, 2)
+        load_words(w3_codes, w3_words, 0, 2)
+        load_scales(w2_plane, w2_scales)
+        load_words(w2_codes, w2_words, 0, E)
+        load_words(w1_codes, w1_words, 2, 4)
+        load_words(w3_codes, w3_words, 2, 4)
+        nc.sync.dma_start(out=gates[:], in_=gate)
+        load_words(w1_codes, w1_words, 4, 8)
+        load_words(w3_codes, w3_words, 4, 8)
+        nc.sync.dma_start(out=residual[:], in_=xr)
+
+        x_codes = [slot_pool.tile([P, SLICE], U32, name="x_codes", align_bytes=64) for s in range(slices)]
+        x_scales = [slot_pool.tile([P, SLICE], U8, name="x_scales", align_bytes=64) for s in range(slices)]
+
+        def gather_second(s):
+            gather(s, 1, gathered[s])
+
+        def quantise_x(s, pieces):
+            grouped = slot_pool.tile([P, 4 * SLICE], BF16, name="grouped", align_bytes=64)
+            src = gathered[s][:].bitcast(F32).rearrange("p (u t) -> p t u", u=2)
+            dst = grouped[:].bitcast(F32).rearrange("p (t u) -> p t u", u=2)
+            step = SLICE // pieces
+            for a in range(0, SLICE, step):
+                nc.scalar.copy(out=dst[:, a : a + step, :], in_=src[:, a : a + step, :])
+                nc.vector.quantize_mx(
+                    out=x_codes[s][:, a : a + step].bitcast(FP8X4),
+                    scales=x_scales[s][:, a : a + step],
+                    in_=grouped[:, 4 * a : 4 * (a + step)],
+                )
+
+        def expert(e, y_bank):
+            s = e // 2
+            turned = psum_t.tile([P, 4 * P], F32, name="turned")
+            for half in range(2):
+                cols = slice((e % 2) * C + half * P, (e % 2) * C + half * P + P)
+                banks = []
+                for pool, codes, plane, name in (
+                    (psum_a, w1_codes, w1_plane, "a_bank"),
+                    (psum_b, w3_codes, w3_plane, "b_bank"),
+                ):
+                    bank = pool.tile([P, H], F32, name=name)
+                    nc.tensor.matmul_mx(
+                        out=bank[:],
+                        lhsT=x_codes[s][:, cols].bitcast(FP8X4),
+                        lhsT_scale=x_scales[s][:, cols],
+                        rhs=codes[:, e * 2 * H : (e + 1) * 2 * H].bitcast(FP4X4),
+                        rhs_scale=plane[:, e * H : (e + 1) * H],
+                        start=True,
+                        stop=True,
+                    )
+                    banks.append(bank)
+                act = work.tile([P, H], F32, name="act")
+                nc.scalar.activation(
+                    act[:].rearrange("s (u p e) -> s u p e", u=2, e=2),
+                    banks[0][:].rearrange("s (p u e) -> s u p e", u=2, e=2),
+                    GELU,
+                )
+                hidden = work.tile([P, H], BF16, name="hidden", align_bytes=64)
+                nc.vector.tensor_tensor(
+                    hidden[:].rearrange("s (u p e) -> s u p e", u=2, e=2),
+                    banks[1][:].rearrange("s (p u e) -> s u p e", u=2, e=2),
+                    act[:].rearrange("s (u p e) -> s u p e", u=2, e=2),
+                    MULT,
+                )
+                words = hidden[:].bitcast(F32)
+                for u in range(2):
+                    place = (2 * half + u) * P
+                    nc.tensor.transpose(turned[:, place : place + P], words[:, u * P : (u + 1) * P], identity[:])
+            h_grouped = work.tile([P, 4 * C], BF16, name="h_grouped", align_bytes=64)
+            nc.scalar.copy(
+                out=h_grouped[:].bitcast(F32).rearrange("p (c r u) -> p c r u", c=2, u=2),
+                in_=turned[:].rearrange("p (c u r) -> p c r u", c=2, u=2),
+            )
+            h_codes = work.tile([P, C], U32, name="h_codes", align_bytes=64)
+            h_scales = work.tile([P, C], U8, name="h_scales", align_bytes=64)
+            nc.vector.quantize_mx(out=h_codes[:].bitcast(FP8X4), scales=h_scales[:], in_=h_grouped[:])
+            nc.tensor.matmul_mx(
+                out=y_bank[:, (e % 2) * C : (e % 2 + 1) * C],
+                lhsT=w2_codes[:, e * 2 * N : (e + 1) * 2 * N].bitcast(FP4X4),
+                lhsT_scale=w2_plane[:, e * N : (e + 1) * N],
+                rhs=h_codes[:].bitcast(FP8X4),
+                rhs_scale=h_scales[:],
+                start=True,
+                stop=True,
+            )
+
+        def scatter(s, results):
+            nc.vector.tensor_tensor(
+                scattered[:].indirect(offsets[:, s * (SLICE // 16) : (s + 1) * (SLICE // 16)]),
+                results[:],
+                gates[:, s * SLICE : (s + 1) * SLICE],
+                MULT,
+            )
+
+        gather_second(0)
+        gather_second(1)
+        quantise_x(0, 2)
+        gather_second(2)
+        quantise_x(1, 1)
+        gather_second(3)
+        quantise_x(2, 1)
+        quantise_x(3, 1)
+        results = []
+        for s in range(slices):
+            y_bank = psum_y.tile([P, SLICE], F32, name="y_bank")
+            expert(2 * s, y_bank)
+            expert(2 * s + 1, y_bank)
+            results.append(work.tile([P, SLICE], F32, name="results"))
+            nc.scalar.copy(out=results[s][:], in_=y_bank[:])
+        for s in range(slices):
+            scatter(s, results[s])
+
+        bounds = [0, 1024, 2048, 2688, T]
+        for c0, c1 in zip(bounds[:-1], bounds[1:]):
+            nc.vector.tensor_tensor(residual[:, c0:c1], residual[:, c0:c1], scattered[:, c0:c1], ADD)
+            nc.sync.dma_start(out=out[:, c0:c1], in_=residual[:, c0:c1])

@@ -34,6 +34,7 @@ def tile_moe_res_glu_gelu_kernel(
         raw_pool = ctx.enter_context(tc.tile_pool(name="raw", bufs=5))
         slot_pool = ctx.enter_context(tc.tile_pool(name="slots", bufs=4))
         work = ctx.enter_context(tc.tile_pool(name="work", bufs=4))
+        act_pool = ctx.enter_context(tc.tile_pool(name="acts", bufs=6))
         psum_a = ctx.enter_context(tc.psum_pool(name="psum_a", bufs=2))
         psum_b = ctx.enter_context(tc.psum_pool(name="psum_b", bufs=4))
         psum_t = ctx.enter_context(tc.psum_pool(name="psum_t", bufs=1))
@@ -71,9 +72,10 @@ def tile_moe_res_glu_gelu_kernel(
             if split < width:
                 nc.vector.tensor_copy(out=dst[:, c0 + split : c1, :], in_=source[:, split:width, :])
 
-        def gather(s, u, dest):
+        def gather(s, u):
+            at = (2 * s + u) * 2 * SLICE
             nc.vector.tensor_copy(
-                dest[:, u * 2 * SLICE : (u + 1) * 2 * SLICE].bitcast(U32),
+                gathered[:, at : at + 2 * SLICE].bitcast(U32),
                 pairs[u][:].bitcast(U32).indirect(offsets[:, s * (SLICE // 16) : (s + 1) * (SLICE // 16)]),
             )
 
@@ -81,9 +83,9 @@ def tile_moe_res_glu_gelu_kernel(
         nc.sync.dma_start(offsets[:], offs)
         load_and_cast(0, 1024, 2048, 512)
         load_and_cast(0, 2048, 3072, 384)
-        gathered = [slot_pool.tile([P, 4 * SLICE], BF16, name="gathered", align_bytes=64) for s in range(slices)]
+        gathered = keep.tile([P, slices * 4 * SLICE], BF16, name="gathered", align_bytes=64)
         for s in range(slices):
-            gather(s, 0, gathered[s])
+            gather(s, 0)
         load_and_cast(1, 0, 1024, 1024)
         load_and_cast(1, 1024, 2048, 1024)
         load_and_cast(1, 2048, 2816, 0)
@@ -119,104 +121,131 @@ def tile_moe_res_glu_gelu_kernel(
 
         x_codes = [slot_pool.tile([P, SLICE], U32, name="x_codes", align_bytes=64) for s in range(slices)]
         x_scales = [slot_pool.tile([P, SLICE], U8, name="x_scales", align_bytes=64) for s in range(slices)]
+        a_banks, b_banks, acts, hiddens, turned, h_grouped, h_codes, h_scales, y_banks, results = ({} for i in range(10))
 
-        def gather_second(s):
-            gather(s, 1, gathered[s])
-
-        def quantise_x(s, pieces):
-            grouped = slot_pool.tile([P, 4 * SLICE], BF16, name="grouped", align_bytes=64)
-            src = gathered[s][:].bitcast(F32).rearrange("p (u t) -> p t u", u=2)
-            dst = grouped[:].bitcast(F32).rearrange("p (t u) -> p t u", u=2)
-            step = SLICE // pieces
-            for a in range(0, SLICE, step):
-                nc.scalar.copy(out=dst[:, a : a + step, :], in_=src[:, a : a + step, :])
-                nc.vector.quantize_mx(
-                    out=x_codes[s][:, a : a + step].bitcast(FP8X4),
-                    scales=x_scales[s][:, a : a + step],
-                    in_=grouped[:, 4 * a : 4 * (a + step)],
-                )
-
-        def expert(e, y_bank):
-            s = e // 2
-            turned = psum_t.tile([P, 4 * P], F32, name="turned")
-            for half in range(2):
-                cols = slice((e % 2) * C + half * P, (e % 2) * C + half * P + P)
-                banks = []
-                for pool, codes, plane, name in (
-                    (psum_a, w1_codes, w1_plane, "a_bank"),
-                    (psum_b, w3_codes, w3_plane, "b_bank"),
-                ):
-                    bank = pool.tile([P, H], F32, name=name)
-                    nc.tensor.matmul_mx(
-                        out=bank[:],
-                        lhsT=x_codes[s][:, cols].bitcast(FP8X4),
-                        lhsT_scale=x_scales[s][:, cols],
-                        rhs=codes[:, e * 2 * H : (e + 1) * 2 * H].bitcast(FP4X4),
-                        rhs_scale=plane[:, e * H : (e + 1) * H],
-                        start=True,
-                        stop=True,
-                    )
-                    banks.append(bank)
-                act = work.tile([P, H], F32, name="act")
-                nc.scalar.activation(
-                    act[:].rearrange("s (u p e) -> s u p e", u=2, e=2),
-                    banks[0][:].rearrange("s (p u e) -> s u p e", u=2, e=2),
-                    GELU,
-                )
-                hidden = work.tile([P, H], BF16, name="hidden", align_bytes=64)
-                nc.vector.tensor_tensor(
-                    hidden[:].rearrange("s (u p e) -> s u p e", u=2, e=2),
-                    banks[1][:].rearrange("s (p u e) -> s u p e", u=2, e=2),
-                    act[:].rearrange("s (u p e) -> s u p e", u=2, e=2),
-                    MULT,
-                )
-                words = hidden[:].bitcast(F32)
-                for u in range(2):
-                    place = (2 * half + u) * P
-                    nc.tensor.transpose(turned[:, place : place + P], words[:, u * P : (u + 1) * P], identity[:])
-            h_grouped = work.tile([P, 4 * C], BF16, name="h_grouped", align_bytes=64)
-            nc.scalar.copy(
-                out=h_grouped[:].bitcast(F32).rearrange("p (c r u) -> p c r u", c=2, u=2),
-                in_=turned[:].rearrange("p (c u r) -> p c r u", c=2, u=2),
+        def quantise_tokens(e):
+            s, at = e // 2, (e % 2) * C
+            src = gathered[:, s * 4 * SLICE : (s + 1) * 4 * SLICE].bitcast(F32).rearrange("p (u t) -> p t u", u=2)
+            if e < 2:
+                place = (2 * (e + 2) + 1) * 2 * SLICE
+                grouped = gathered[:, place : place + 4 * C]
+            else:
+                grouped = slot_pool.tile([P, 4 * C], BF16, name="grouped", align_bytes=64)[:]
+            nc.scalar.copy(out=grouped.bitcast(F32).rearrange("p (t u) -> p t u", u=2), in_=src[:, at : at + C, :])
+            nc.vector.quantize_mx(
+                out=x_codes[s][:, at : at + C].bitcast(FP8X4),
+                scales=x_scales[s][:, at : at + C],
+                in_=grouped,
             )
-            h_codes = work.tile([P, C], U32, name="h_codes", align_bytes=64)
-            h_scales = work.tile([P, C], U8, name="h_scales", align_bytes=64)
-            nc.vector.quantize_mx(out=h_codes[:].bitcast(FP8X4), scales=h_scales[:], in_=h_grouped[:])
+
+        def first_products(c):
+            e, s, at = c // 2, c // 4, (c % 4) * P
+            for banks, pool, codes, plane, name in (
+                (a_banks, psum_a, w1_codes, w1_plane, "a_bank"),
+                (b_banks, psum_b, w3_codes, w3_plane, "b_bank"),
+            ):
+                banks[c] = pool.tile([P, H], F32, name=name)
+                nc.tensor.matmul_mx(
+                    out=banks[c][:],
+                    lhsT=x_codes[s][:, at : at + P].bitcast(FP8X4),
+                    lhsT_scale=x_scales[s][:, at : at + P],
+                    rhs=codes[:, e * 2 * H : (e + 1) * 2 * H].bitcast(FP4X4),
+                    rhs_scale=plane[:, e * H : (e + 1) * H],
+                    start=True,
+                    stop=True,
+                )
+
+        def activate(c):
+            acts[c] = act_pool.tile([P, H], F32, name="act")
+            nc.scalar.activation(
+                acts[c][:].rearrange("s (u p e) -> s u p e", u=2, e=2),
+                a_banks[c][:].rearrange("s (p u e) -> s u p e", u=2, e=2),
+                GELU,
+            )
+
+        def multiply(c):
+            hiddens[c] = work.tile([P, H], BF16, name="hidden", align_bytes=64)
+            nc.vector.tensor_tensor(
+                hiddens[c][:].rearrange("s (u p e) -> s u p e", u=2, e=2),
+                b_banks[c][:].rearrange("s (p u e) -> s u p e", u=2, e=2),
+                acts[c][:].rearrange("s (u p e) -> s u p e", u=2, e=2),
+                MULT,
+            )
+
+        def turn(c):
+            if c % 2 == 0:
+                turned[c // 2] = psum_t.tile([P, 4 * P], F32, name="turned")
+            words = hiddens[c][:].bitcast(F32)
+            for u in range(2):
+                place = (2 * (c % 2) + u) * P
+                nc.tensor.transpose(turned[c // 2][:, place : place + P], words[:, u * P : (u + 1) * P], identity[:])
+
+        def group_hidden(e):
+            h_grouped[e] = work.tile([P, 4 * C], BF16, name="h_grouped", align_bytes=64)
+            nc.scalar.copy(
+                out=h_grouped[e][:].bitcast(F32).rearrange("p (c r u) -> p c r u", c=2, u=2),
+                in_=turned[e][:].rearrange("p (c u r) -> p c r u", c=2, u=2),
+            )
+
+        def quantise_hidden(e):
+            h_codes[e] = work.tile([P, C], U32, name="h_codes", align_bytes=64)
+            h_scales[e] = work.tile([P, C], U8, name="h_scales", align_bytes=64)
+            nc.vector.quantize_mx(out=h_codes[e][:].bitcast(FP8X4), scales=h_scales[e][:], in_=h_grouped[e][:])
+
+        def second_product(e):
+            if e % 2 == 0:
+                y_banks[e // 2] = psum_y.tile([P, SLICE], F32, name="y_bank")
             nc.tensor.matmul_mx(
-                out=y_bank[:, (e % 2) * C : (e % 2 + 1) * C],
+                out=y_banks[e // 2][:, (e % 2) * C : (e % 2 + 1) * C],
                 lhsT=w2_codes[:, e * 2 * N : (e + 1) * 2 * N].bitcast(FP4X4),
                 lhsT_scale=w2_plane[:, e * N : (e + 1) * N],
-                rhs=h_codes[:].bitcast(FP8X4),
-                rhs_scale=h_scales[:],
+                rhs=h_codes[e][:].bitcast(FP8X4),
+                rhs_scale=h_scales[e][:],
                 start=True,
                 stop=True,
             )
 
-        def scatter(s, results):
+        def collect(s):
+            results[s] = work.tile([P, SLICE], F32, name="results")
+            nc.scalar.copy(out=results[s][:], in_=y_banks[s][:])
+
+        def scatter(s):
             nc.vector.tensor_tensor(
                 scattered[:].indirect(offsets[:, s * (SLICE // 16) : (s + 1) * (SLICE // 16)]),
-                results[:],
+                results[s][:],
                 gates[:, s * SLICE : (s + 1) * SLICE],
                 MULT,
             )
 
-        gather_second(0)
-        gather_second(1)
-        quantise_x(0, 2)
-        gather_second(2)
-        quantise_x(1, 1)
-        gather_second(3)
-        quantise_x(2, 1)
-        quantise_x(3, 1)
-        results = []
-        for s in range(slices):
-            y_bank = psum_y.tile([P, SLICE], F32, name="y_bank")
-            expert(2 * s, y_bank)
-            expert(2 * s + 1, y_bank)
-            results.append(work.tile([P, SLICE], F32, name="results"))
-            nc.scalar.copy(out=results[s][:], in_=y_bank[:])
-        for s in range(slices):
-            scatter(s, results[s])
+        gather(0, 1)
+        gather(1, 1)
+        quantise_tokens(0)
+        quantise_tokens(1)
+        gather(2, 1)
+        gather(3, 1)
+        chunks = S // P
+        scatter_at = (12, 14, 18, 23)
+        for c in range(-2, max(scatter_at) + 1):
+            if (c + 5) % 2 == 0 and 2 <= (c + 5) // 2 < E:
+                quantise_tokens((c + 5) // 2)
+            if 0 <= c + 2 < chunks:
+                first_products(c + 2)
+            if 0 <= c + 1 < chunks:
+                activate(c + 1)
+            if 0 <= c < chunks:
+                multiply(c)
+            if 0 <= c - 1 < chunks:
+                turn(c - 1)
+            if (c - 1) % 2 == 1 and 0 < c - 1 < chunks:
+                group_hidden((c - 1) // 2)
+            if (c - 2) % 2 == 1 and 0 < c - 2 < chunks:
+                quantise_hidden((c - 2) // 2)
+            if (c - 4) % 2 == 1 and 0 < c - 4 < chunks:
+                second_product((c - 4) // 2)
+            if (c - 5) % 4 == 3 and 0 < c - 5 < chunks:
+                collect((c - 5) // 4)
+            if c in scatter_at:
+                scatter(scatter_at.index(c))
 
         bounds = [0, 1024, 2048, 2688, T]
         for c0, c1 in zip(bounds[:-1], bounds[1:]):

@@ -31,14 +31,11 @@ def tile_moe_res_glu_gelu_kernel(
 
     with ExitStack() as ctx:
         keep = ctx.enter_context(tc.tile_pool(name="keep", bufs=1))
-        raw_pool = ctx.enter_context(tc.tile_pool(name="raw", bufs=5))
+        raw_pool = ctx.enter_context(tc.tile_pool(name="raw", bufs=7))
         slot_pool = ctx.enter_context(tc.tile_pool(name="slots", bufs=4))
         work = ctx.enter_context(tc.tile_pool(name="work", bufs=4))
         act_pool = ctx.enter_context(tc.tile_pool(name="acts", bufs=6))
-        psum_a = ctx.enter_context(tc.psum_pool(name="psum_a", bufs=2))
-        psum_b = ctx.enter_context(tc.psum_pool(name="psum_b", bufs=4))
-        psum_t = ctx.enter_context(tc.psum_pool(name="psum_t", bufs=1))
-        psum_y = ctx.enter_context(tc.psum_pool(name="psum_y", bufs=1))
+        psum = ctx.enter_context(tc.psum_pool(name="psum", bufs=8))
 
         offsets = keep.tile([P, S // 16], U16, name="offsets")
         pairs = [keep.tile([P, 2 * T], BF16, name=f"pairs{u}", align_bytes=64) for u in range(2)]
@@ -55,11 +52,11 @@ def tile_moe_res_glu_gelu_kernel(
         warm = keep.tile([P, 1], F32, name="warm")
 
         nc.vector.memset(warm[:], 0.0)
+        nc.vector.memset(scattered[:], 0.0)
         nc.scalar.activation(warm[:], warm[:], GELU)
         for plane in (w1_plane, w3_plane, w2_plane):
             nc.gpsimd.memset(plane[:].bitcast(I32), 0)
         make_identity(nc, identity[:])
-        nc.gpsimd.memset(scattered[:], 0.0)
 
         def load_and_cast(u, c0, c1, split):
             width = c1 - c0
@@ -72,11 +69,10 @@ def tile_moe_res_glu_gelu_kernel(
             if split < width:
                 nc.vector.tensor_copy(out=dst[:, c0 + split : c1, :], in_=source[:, split:width, :])
 
-        def gather(s, u):
-            at = (2 * s + u) * 2 * SLICE
+        def gather(u, first, last):
             nc.vector.tensor_copy(
-                gathered[:, at : at + 2 * SLICE].bitcast(U32),
-                pairs[u][:].bitcast(U32).indirect(offsets[:, s * (SLICE // 16) : (s + 1) * (SLICE // 16)]),
+                gathered[:, 2 * (u * S + first) : 2 * (u * S + last)].bitcast(U32),
+                pairs[u][:].bitcast(U32).indirect(offsets[:, first // 16 : last // 16]),
             )
 
         load_and_cast(0, 0, 1024, 512)
@@ -84,18 +80,19 @@ def tile_moe_res_glu_gelu_kernel(
         load_and_cast(0, 1024, 2048, 512)
         load_and_cast(0, 2048, 3072, 384)
         gathered = keep.tile([P, slices * 4 * SLICE], BF16, name="gathered", align_bytes=64)
-        for s in range(slices):
-            gather(s, 0)
+        for first in range(0, S, S // 4):
+            gather(0, first, first + S // 4)
         load_and_cast(1, 0, 1024, 1024)
         load_and_cast(1, 1024, 2048, 1024)
         load_and_cast(1, 2048, 2816, 0)
         load_and_cast(1, 2816, 3072, 0)
 
-        def load_scales(plane, scales):
-            rows = scales.rearrange("e s (q r) i -> r q (e s) i", r=4)
+        def load_scales(plane, scales, e0, e1):
+            wide = scales.shape[3]
+            rows = scales[e0:e1].rearrange("e s (q r) i -> r q (e s) i", r=4)
             for r in range(4):
                 nc.sync.dma_start(
-                    out=plane[r:P:32, :].bitcast(I32).rearrange("q (e i) -> q e i", e=E),
+                    out=plane[r:P:32, e0 * wide : e1 * wide].bitcast(I32).rearrange("q (e i) -> q e i", e=e1 - e0),
                     in_=rows[r].bitcast(I32),
                 )
 
@@ -106,45 +103,50 @@ def tile_moe_res_glu_gelu_kernel(
                 in_=words[e0:e1].rearrange("e s p b -> p (e s) b").bitcast(I32),
             )
 
-        load_scales(w1_plane, w1_scales)
-        load_scales(w3_plane, w3_scales)
+        load_scales(w1_plane, w1_scales, 0, 2)
+        load_scales(w3_plane, w3_scales, 0, 2)
         load_words(w1_codes, w1_words, 0, 2)
         load_words(w3_codes, w3_words, 0, 2)
-        load_scales(w2_plane, w2_scales)
-        load_words(w2_codes, w2_words, 0, E)
         load_words(w1_codes, w1_words, 2, 4)
         load_words(w3_codes, w3_words, 2, 4)
+        load_scales(w1_plane, w1_scales, 2, E)
+        load_scales(w3_plane, w3_scales, 2, E)
+        load_scales(w2_plane, w2_scales, 0, E)
+        load_words(w2_codes, w2_words, 0, E)
         nc.sync.dma_start(out=gates[:], in_=gate)
-        load_words(w1_codes, w1_words, 4, 8)
-        load_words(w3_codes, w3_words, 4, 8)
+        load_words(w1_codes, w1_words, 4, E)
+        load_words(w3_codes, w3_words, 4, E)
         nc.sync.dma_start(out=residual[:], in_=xr)
 
         x_codes = [slot_pool.tile([P, SLICE], U32, name="x_codes", align_bytes=64) for s in range(slices)]
         x_scales = [slot_pool.tile([P, SLICE], U8, name="x_scales", align_bytes=64) for s in range(slices)]
         a_banks, b_banks, acts, hiddens, turned, h_grouped, h_codes, h_scales, y_banks, results = ({} for i in range(10))
 
+        by_pair = gathered[:].bitcast(F32).rearrange("p (u t) -> p t u", u=2)
+
         def quantise_tokens(e):
             s, at = e // 2, (e % 2) * C
-            src = gathered[:, s * 4 * SLICE : (s + 1) * 4 * SLICE].bitcast(F32).rearrange("p (u t) -> p t u", u=2)
+            width = C
             if e < 2:
-                place = (2 * (e + 2) + 1) * 2 * SLICE
-                grouped = gathered[:, place : place + 4 * C]
+                place = 2 * S + 2 * (e + 2) * SLICE
+                grouped = gathered[:, place : place + 4 * width]
             else:
-                grouped = slot_pool.tile([P, 4 * C], BF16, name="grouped", align_bytes=64)[:]
-            nc.scalar.copy(out=grouped.bitcast(F32).rearrange("p (t u) -> p t u", u=2), in_=src[:, at : at + C, :])
+                grouped = slot_pool.tile([P, 4 * width], BF16, name="grouped", align_bytes=64)[:]
+            engine_copy = nc.scalar.copy if e < 4 else nc.vector.tensor_copy
+            engine_copy(
+                out=grouped.bitcast(F32).rearrange("p (t u) -> p t u", u=2),
+                in_=by_pair[:, e * C : e * C + width, :],
+            )
             nc.vector.quantize_mx(
-                out=x_codes[s][:, at : at + C].bitcast(FP8X4),
-                scales=x_scales[s][:, at : at + C],
+                out=x_codes[s][:, at : at + width].bitcast(FP8X4),
+                scales=x_scales[s][:, at : at + width],
                 in_=grouped,
             )
 
         def first_products(c):
             e, s, at = c // 2, c // 4, (c % 4) * P
-            for banks, pool, codes, plane, name in (
-                (a_banks, psum_a, w1_codes, w1_plane, "a_bank"),
-                (b_banks, psum_b, w3_codes, w3_plane, "b_bank"),
-            ):
-                banks[c] = pool.tile([P, H], F32, name=name)
+            for banks, codes, plane in ((a_banks, w1_codes, w1_plane), (b_banks, w3_codes, w3_plane)):
+                banks[c] = psum.tile([P, H], F32, name="bank")
                 nc.tensor.matmul_mx(
                     out=banks[c][:],
                     lhsT=x_codes[s][:, at : at + P].bitcast(FP8X4),
@@ -174,7 +176,7 @@ def tile_moe_res_glu_gelu_kernel(
 
         def turn(c):
             if c % 2 == 0:
-                turned[c // 2] = psum_t.tile([P, 4 * P], F32, name="turned")
+                turned[c // 2] = psum.tile([P, 4 * P], F32, name="bank")
             words = hiddens[c][:].bitcast(F32)
             for u in range(2):
                 place = (2 * (c % 2) + u) * P
@@ -194,7 +196,7 @@ def tile_moe_res_glu_gelu_kernel(
 
         def second_product(e):
             if e % 2 == 0:
-                y_banks[e // 2] = psum_y.tile([P, SLICE], F32, name="y_bank")
+                y_banks[e // 2] = psum.tile([P, SLICE], F32, name="bank")
             nc.tensor.matmul_mx(
                 out=y_banks[e // 2][:, (e % 2) * C : (e % 2 + 1) * C],
                 lhsT=w2_codes[:, e * 2 * N : (e + 1) * 2 * N].bitcast(FP4X4),
@@ -217,19 +219,19 @@ def tile_moe_res_glu_gelu_kernel(
                 MULT,
             )
 
-        gather(0, 1)
-        gather(1, 1)
+        gather(1, 0 * SLICE, 1 * SLICE)
+        gather(1, 1 * SLICE, 2 * SLICE)
         quantise_tokens(0)
         quantise_tokens(1)
-        gather(2, 1)
-        gather(3, 1)
+        gather(1, 2 * SLICE, 3 * SLICE)
+        gather(1, 3 * SLICE, 4 * SLICE)
         chunks = S // P
         scatter_at = (12, 14, 18, 23)
-        for c in range(-2, max(scatter_at) + 1):
+        for c in range(-3, max(scatter_at) + 1):
             if (c + 5) % 2 == 0 and 2 <= (c + 5) // 2 < E:
                 quantise_tokens((c + 5) // 2)
-            if 0 <= c + 2 < chunks:
-                first_products(c + 2)
+            if 0 <= c + 3 < chunks:
+                first_products(c + 3)
             if 0 <= c + 1 < chunks:
                 activate(c + 1)
             if 0 <= c < chunks:

@@ -31,7 +31,7 @@ def tile_moe_res_glu_gelu_kernel(
 
     with ExitStack() as ctx:
         keep = ctx.enter_context(tc.tile_pool(name="keep", bufs=1))
-        raw_pool = ctx.enter_context(tc.tile_pool(name="raw", bufs=7))
+        raw_pool = ctx.enter_context(tc.tile_pool(name="raw", bufs=1))
         slot_pool = ctx.enter_context(tc.tile_pool(name="slots", bufs=4))
         work = ctx.enter_context(tc.tile_pool(name="work", bufs=4))
         act_pool = ctx.enter_context(tc.tile_pool(name="acts", bufs=6))
@@ -60,7 +60,7 @@ def tile_moe_res_glu_gelu_kernel(
 
         def load_and_cast(u, c0, c1, split):
             width = c1 - c0
-            raw = raw_pool.tile([P, 2, width], F32, name="raw")
+            raw = raw_pool.tile([P, 2, width], F32, name=f"raw{u}_{c0}")
             nc.sync.dma_start(out=raw[:], in_=x_rows[:, 2 * u : 2 * u + 2, c0:c1])
             dst = pairs[u][:].rearrange("p (t e) -> p t e", e=2)
             source = raw[:].rearrange("p e t -> p t e")
@@ -75,13 +75,12 @@ def tile_moe_res_glu_gelu_kernel(
                 pairs[u][:].bitcast(U32).indirect(offsets[:, first // 16 : last // 16]),
             )
 
-        load_and_cast(0, 0, 1024, 512)
+        load_and_cast(0, 0, 2048, 896)
         nc.sync.dma_start(offsets[:], offs)
-        load_and_cast(0, 1024, 2048, 512)
         load_and_cast(0, 2048, 3072, 384)
         gathered = keep.tile([P, slices * 4 * SLICE], BF16, name="gathered", align_bytes=64)
-        for first in range(0, S, S // 4):
-            gather(0, first, first + S // 4)
+        for first in range(0, S, S // 2):
+            gather(0, first, first + S // 2)
         load_and_cast(1, 0, 1024, 1024)
         load_and_cast(1, 1024, 2048, 1024)
         load_and_cast(1, 2048, 2816, 0)
@@ -104,8 +103,8 @@ def tile_moe_res_glu_gelu_kernel(
             )
 
         load_scales(w1_plane, w1_scales, 0, 2)
-        load_scales(w3_plane, w3_scales, 0, 2)
         load_words(w1_codes, w1_words, 0, 2)
+        load_scales(w3_plane, w3_scales, 0, 2)
         load_words(w3_codes, w3_words, 0, 2)
         load_words(w1_codes, w1_words, 2, 4)
         load_words(w3_codes, w3_words, 2, 4)
@@ -126,14 +125,13 @@ def tile_moe_res_glu_gelu_kernel(
 
         def quantise_tokens(e):
             s, at = e // 2, (e % 2) * C
-            width = C
+            width = C if e < 4 else SLICE
             if e < 2:
                 place = 2 * S + 2 * (e + 2) * SLICE
                 grouped = gathered[:, place : place + 4 * width]
             else:
                 grouped = slot_pool.tile([P, 4 * width], BF16, name="grouped", align_bytes=64)[:]
-            engine_copy = nc.scalar.copy if e < 4 else nc.vector.tensor_copy
-            engine_copy(
+            nc.scalar.copy(
                 out=grouped.bitcast(F32).rearrange("p (t u) -> p t u", u=2),
                 in_=by_pair[:, e * C : e * C + width, :],
             )
@@ -228,7 +226,7 @@ def tile_moe_res_glu_gelu_kernel(
         chunks = S // P
         scatter_at = (12, 14, 18, 23)
         for c in range(-3, max(scatter_at) + 1):
-            if (c + 5) % 2 == 0 and 2 <= (c + 5) // 2 < E:
+            if c in (-1, 1, 3, 7):
                 quantise_tokens((c + 5) // 2)
             if 0 <= c + 3 < chunks:
                 first_products(c + 3)
@@ -249,7 +247,7 @@ def tile_moe_res_glu_gelu_kernel(
             if c in scatter_at:
                 scatter(scatter_at.index(c))
 
-        bounds = [0, 1024, 2048, 2688, T]
+        bounds = [0, 640, 1280, 1920, 2560, T]
         for c0, c1 in zip(bounds[:-1], bounds[1:]):
             nc.vector.tensor_tensor(residual[:, c0:c1], residual[:, c0:c1], scattered[:, c0:c1], ADD)
             nc.sync.dma_start(out=out[:, c0:c1], in_=residual[:, c0:c1])

from contextlib import ExitStack

import concourse.mybir as mybir
from concourse.masks import make_identity

F32 = mybir.dt.float32
BF16 = mybir.dt.bfloat16
I32 = mybir.dt.int32
U32 = mybir.dt.uint32
U16 = mybir.dt.uint16
U8 = mybir.dt.uint8
FP8X4 = mybir.dt.float8_e4m3fn_x4
FP4X4 = mybir.dt.float4_e2m1fn_x4
GELU = mybir.ActivationFunctionType.Gelu_apprx_tanh
MULT = mybir.AluOpType.mult
ADD = mybir.AluOpType.add

P = 128
K, T, E, C, H, N = 512, 3072, 8, 256, 512, 128
S = E * C
SLICE = 512
FLOPS = 2 * S * (2 * K * H + H * N)


def tile_moe_res_glu_gelu_kernel(
    tc, xT, xr, w1_words, w1_scales, w3_words, w3_scales, w2_words, w2_scales, gate, offs, out
):
    nc = tc.nc
    x_rows = xT.rearrange("(p j) t -> p j t", j=4)
    slices = S // SLICE

    with ExitStack() as ctx:
        keep = ctx.enter_context(tc.tile_pool(name="keep", bufs=1))
        raw_pool = ctx.enter_context(tc.tile_pool(name="raw", bufs=1))
        slot_pool = ctx.enter_context(tc.tile_pool(name="slots", bufs=4))
        work = ctx.enter_context(tc.tile_pool(name="work", bufs=4))
        act_pool = ctx.enter_context(tc.tile_pool(name="acts", bufs=6))
        psum = ctx.enter_context(tc.psum_pool(name="psum", bufs=8))

        offsets = keep.tile([P, S // 16], U16, name="offsets")
        pairs = [keep.tile([P, 2 * T], BF16, name=f"pairs{u}", align_bytes=64) for u in range(2)]
        w1_codes = keep.tile([P, E * 2 * H], U8, name="w1_codes", align_bytes=64)
        w3_codes = keep.tile([P, E * 2 * H], U8, name="w3_codes", align_bytes=64)
        w2_codes = keep.tile([P, E * 2 * N], U8, name="w2_codes", align_bytes=64)
        w1_plane = keep.tile([P, E * H], U8, name="w1_plane", align_bytes=64)
        w3_plane = keep.tile([P, E * H], U8, name="w3_plane", align_bytes=64)
        w2_plane = keep.tile([P, E * N], U8, name="w2_plane", align_bytes=64)
        gates = keep.tile([P, S], F32, name="gates")
        residual = keep.tile([P, T], F32, name="residual")
        scattered = keep.tile([P, T], F32, name="scattered")
        identity = keep.tile([P, P], F32, name="identity")
        warm = keep.tile([P, 1], F32, name="warm")

        nc.vector.memset(warm[:], 0.0)
        nc.vector.memset(scattered[:], 0.0)
        nc.scalar.activation(warm[:], warm[:], GELU)
        for plane in (w1_plane, w3_plane, w2_plane):
            nc.gpsimd.memset(plane[:].bitcast(I32), 0)
        make_identity(nc, identity[:])

        def load_and_cast(u, c0, c1, split):
            width = c1 - c0
            raw = raw_pool.tile([P, 2, width], F32, name=f"raw{u}_{c0}")
            nc.sync.dma_start(out=raw[:], in_=x_rows[:, 2 * u : 2 * u + 2, c0:c1])
            dst = pairs[u][:].rearrange("p (t e) -> p t e", e=2)
            source = raw[:].rearrange("p e t -> p t e")
            if split > 0:
                nc.scalar.copy(out=dst[:, c0 : c0 + split, :], in_=source[:, 0:split, :])
            if split < width:
                nc.vector.tensor_copy(out=dst[:, c0 + split : c1, :], in_=source[:, split:width, :])

        def gather(u, first, last):
            nc.vector.tensor_copy(
                gathered[:, 2 * (u * S + first) : 2 * (u * S + last)].bitcast(U32),
                pairs[u][:].bitcast(U32).indirect(offsets[:, first // 16 : last // 16]),
            )

        load_and_cast(0, 0, 2048, 896)
        nc.sync.dma_start(offsets[:], offs)
        load_and_cast(0, 2048, 3072, 384)
        gathered = keep.tile([P, slices * 4 * SLICE], BF16, name="gathered", align_bytes=64)
        for first in range(0, S, S // 2):
            gather(0, first, first + S // 2)
        load_and_cast(1, 0, 1024, 1024)
        load_and_cast(1, 1024, 2048, 1024)
        load_and_cast(1, 2048, 2816, 0)
        load_and_cast(1, 2816, 3072, 0)

        def load_scales(plane, scales, e0, e1):
            wide = scales.shape[3]
            rows = scales[e0:e1].rearrange("e s (q r) i -> r q (e s) i", r=4)
            for r in range(4):
                nc.sync.dma_start(
                    out=plane[r:P:32, e0 * wide : e1 * wide].bitcast(I32).rearrange("q (e i) -> q e i", e=e1 - e0),
                    in_=rows[r].bitcast(I32),
                )

        def load_words(codes, words, e0, e1):
            wide = words.shape[3]
            nc.sync.dma_start(
                out=codes[:, e0 * wide : e1 * wide].bitcast(I32).rearrange("p (e b) -> p e b", e=e1 - e0),
                in_=words[e0:e1].rearrange("e s p b -> p (e s) b").bitcast(I32),
            )

        load_scales(w1_plane, w1_scales, 0, 2)
        load_words(w1_codes, w1_words, 0, 2)
        load_scales(w3_plane, w3_scales, 0, 2)
        load_words(w3_codes, w3_words, 0, 2)
        load_words(w1_codes, w1_words, 2, 4)
        load_words(w3_codes, w3_words, 2, 4)
        load_scales(w1_plane, w1_scales, 2, E)
        load_scales(w3_plane, w3_scales, 2, E)
        load_scales(w2_plane, w2_scales, 0, E)
        load_words(w2_codes, w2_words, 0, E)
        nc.sync.dma_start(out=gates[:], in_=gate)
        load_words(w1_codes, w1_words, 4, E)
        load_words(w3_codes, w3_words, 4, E)
        nc.sync.dma_start(out=residual[:], in_=xr)

        x_codes = [slot_pool.tile([P, SLICE], U32, name="x_codes", align_bytes=64) for s in range(slices)]
        x_scales = [slot_pool.tile([P, SLICE], U8, name="x_scales", align_bytes=64) for s in range(slices)]
        a_banks, b_banks, acts, hiddens, turned, h_grouped, h_codes, h_scales, y_banks, results = ({} for i in range(10))

        by_pair = gathered[:].bitcast(F32).rearrange("p (u t) -> p t u", u=2)

        def quantise_tokens(e):
            s, at = e // 2, (e % 2) * C
            width = C if e < 4 else SLICE
            if e < 2:
                place = 2 * S + 2 * (e + 2) * SLICE
                grouped = gathered[:, place : place + 4 * width]
            else:
                grouped = slot_pool.tile([P, 4 * width], BF16, name="grouped", align_bytes=64)[:]
            nc.scalar.copy(
                out=grouped.bitcast(F32).rearrange("p (t u) -> p t u", u=2),
                in_=by_pair[:, e * C : e * C + width, :],
            )
            nc.vector.quantize_mx(
                out=x_codes[s][:, at : at + width].bitcast(FP8X4),
                scales=x_scales[s][:, at : at + width],
                in_=grouped,
            )

        def first_products(c):
            e, s, at = c // 2, c // 4, (c % 4) * P
            for banks, codes, plane in ((a_banks, w1_codes, w1_plane), (b_banks, w3_codes, w3_plane)):
                banks[c] = psum.tile([P, H], F32, name="bank")
                nc.tensor.matmul_mx(
                    out=banks[c][:],
                    lhsT=x_codes[s][:, at : at + P].bitcast(FP8X4),
                    lhsT_scale=x_scales[s][:, at : at + P],
                    rhs=codes[:, e * 2 * H : (e + 1) * 2 * H].bitcast(FP4X4),
                    rhs_scale=plane[:, e * H : (e + 1) * H],
                    start=True,
                    stop=True,
                )

        def activate(c):
            acts[c] = act_pool.tile([P, H], F32, name="act")
            nc.scalar.activation(
                acts[c][:].rearrange("s (u p e) -> s u p e", u=2, e=2),
                a_banks[c][:].rearrange("s (p u e) -> s u p e", u=2, e=2),
                GELU,
            )

        def multiply(c):
            hiddens[c] = work.tile([P, H], BF16, name="hidden", align_bytes=64)
            nc.vector.tensor_tensor(
                hiddens[c][:].rearrange("s (u p e) -> s u p e", u=2, e=2),
                b_banks[c][:].rearrange("s (p u e) -> s u p e", u=2, e=2),
                acts[c][:].rearrange("s (u p e) -> s u p e", u=2, e=2),
                MULT,
            )

        def turn(c):
            if c % 2 == 0:
                turned[c // 2] = psum.tile([P, 4 * P], F32, name="bank")
            words = hiddens[c][:].bitcast(F32)
            for u in range(2):
                place = (2 * (c % 2) + u) * P
                nc.tensor.transpose(turned[c // 2][:, place : place + P], words[:, u * P : (u + 1) * P], identity[:])

        def group_hidden(e):
            h_grouped[e] = work.tile([P, 4 * C], BF16, name="h_grouped", align_bytes=64)
            nc.scalar.copy(
                out=h_grouped[e][:].bitcast(F32).rearrange("p (c r u) -> p c r u", c=2, u=2),
                in_=turned[e][:].rearrange("p (c u r) -> p c r u", c=2, u=2),
            )

        def quantise_hidden(e):
            h_codes[e] = work.tile([P, C], U32, name="h_codes", align_bytes=64)
            h_scales[e] = work.tile([P, C], U8, name="h_scales", align_bytes=64)
            nc.vector.quantize_mx(out=h_codes[e][:].bitcast(FP8X4), scales=h_scales[e][:], in_=h_grouped[e][:])

        def second_product(e):
            if e % 2 == 0:
                y_banks[e // 2] = psum.tile([P, SLICE], F32, name="bank")
            nc.tensor.matmul_mx(
                out=y_banks[e // 2][:, (e % 2) * C : (e % 2 + 1) * C],
                lhsT=w2_codes[:, e * 2 * N : (e + 1) * 2 * N].bitcast(FP4X4),
                lhsT_scale=w2_plane[:, e * N : (e + 1) * N],
                rhs=h_codes[e][:].bitcast(FP8X4),
                rhs_scale=h_scales[e][:],
                start=True,
                stop=True,
            )

        def collect(s):
            results[s] = work.tile([P, SLICE], F32, name="results")
            nc.scalar.copy(out=results[s][:], in_=y_banks[s][:])

        def scatter(s):
            nc.vector.tensor_tensor(
                scattered[:].indirect(offsets[:, s * (SLICE // 16) : (s + 1) * (SLICE // 16)]),
                results[s][:],
                gates[:, s * SLICE : (s + 1) * SLICE],
                MULT,
            )

        gather(1, 0 * SLICE, 1 * SLICE)
        gather(1, 1 * SLICE, 2 * SLICE)
        quantise_tokens(0)
        quantise_tokens(1)
        gather(1, 2 * SLICE, 3 * SLICE)
        gather(1, 3 * SLICE, 4 * SLICE)
        chunks = S // P
        scatter_at = (12, 14, 18, 23)
        for c in range(-3, max(scatter_at) + 1):
            if c in (-1, 1, 3, 7):
                quantise_tokens((c + 5) // 2)
            if 0 <= c + 3 < chunks:
                first_products(c + 3)
            if 0 <= c + 1 < chunks:
                activate(c + 1)
            if 0 <= c < chunks:
                multiply(c)
            if 0 <= c - 1 < chunks:
                turn(c - 1)
            if (c - 1) % 2 == 1 and 0 < c - 1 < chunks:
                group_hidden((c - 1) // 2)
            if (c - 2) % 2 == 1 and 0 < c - 2 < chunks:
                quantise_hidden((c - 2) // 2)
            if (c - 4) % 2 == 1 and 0 < c - 4 < chunks:
                second_product((c - 4) // 2)
            if (c - 5) % 4 == 3 and 0 < c - 5 < chunks:
                collect((c - 5) // 4)
            if c in scatter_at:
                scatter(scatter_at.index(c))

        bounds = [0, 640, 1280, 1920, 2560, T]
        for c0, c1 in zip(bounds[:-1], bounds[1:]):
            nc.vector.tensor_tensor(residual[:, c0:c1], residual[:, c0:c1], scattered[:, c0:c1], ADD)
            nc.sync.dma_start(out=out[:, c0:c1], in_=residual[:, c0:c1])
